import numpy as np
CORES = [68,69,70,71,76,77,78,79,84,85,86,87,92,93,94,95]
N = 16
def setup_inputs(rng):
    return {"x1": rng.standard_normal((N, 128, 3), dtype=np.float32), "x2": rng.standard_normal((N, 128, 1), dtype=np.float32), "x3": rng.standard_normal((N, 128, 4), dtype=np.float32), "x4": rng.standard_normal((N, 128, 2), dtype=np.float32)}
def reference(x1, x2, x3, x4):
    out = {}
    s = x1.sum(axis=0, dtype=np.float64).astype(x1.dtype)
    out["y1"] = np.broadcast_to(s, (N,) + s.shape)
    s = x2.sum(axis=0, dtype=np.float64).astype(x2.dtype)
    out["y2"] = np.broadcast_to(s, (N,) + s.shape)
    s = x3.sum(axis=0, dtype=np.float64).astype(x3.dtype)
    out["y3"] = np.broadcast_to(s, (N,) + s.shape)
    s = x4.sum(axis=0, dtype=np.float64).astype(x4.dtype)
    out["y4"] = np.broadcast_to(s, (N,) + s.shape)
    return out

@@ -1,0 +1,78 @@
+from concourse.bass import DstId, RemoteDMATransfer
+
+ROWS = {"1": (0, 192), "2": (192, 256), "3": (256, 512), "4": (512, 640)}
+CHIPS = (8, 9, 10, 11)
+NP = 5
+LANES = (((0, 1, 2), 2, 0), ((3, 4), 3, 1))
+
+SCRATCH = {
+    "mine": ("dram", [640, 2], "float32"),
+    "slots": ("dram", [4 * NP, 128, 2], "float32"),
+    "part": ("dram", [4 * NP, 128, 2], "float32"),
+    "land": ("dram", [640, 2], "float32"),
+}
+SEMAPHORES = ["loaded", "arr", "parr", "fin", "sent", "stored"]
+
+
+def _dst(topo, c):
+    rid, pid, _se = topo.addr(c)
+    return DstId(rid=rid, pnc=pid)
+
+
+def _piece(buf, p):
+    return buf[p * 128:(p + 1) * 128, :]
+
+
+def rank_program(g, core, T, topo):
+    chip, k = topo.chip(core), core % 8
+    if chip not in CHIPS:
+        return
+    ci = CHIPS.index(chip)
+    mate, plane, diag = chip ^ 1, chip ^ 2, chip ^ 3
+
+    for pieces, a_core, b_core in LANES:
+        if k == a_core:
+            g.wait_ge(T.sem.arr, 4 * len(pieces) * 2)
+            groups = ((diag, chip), (mate, plane)) if len(pieces) == 3 else ((diag,), (mate,), (plane,), (chip,))
+            tr = []
+            for p in pieces:
+                for grp in groups:
+                    tr.append(RemoteDMATransfer(
+                        dst_ids=[_dst(topo, c * 8 + b_core) for c in grp], dma_engine_mask=1 << len(tr),
+                        remote_sem=T.sem.parr, srcs=[T.slots[r * NP + p] for r in range(4)],
+                        dsts=[T.part[ci * NP + p] for c in grp], alu_op=1))
+            g.remote_dma_fused(tr, local_sem=T.sem.sent)
+            g.wait_ge(T.sem.sent, len(tr))
+            return
+        if k == b_core:
+            g.wait_ge(T.sem.parr, 4 * len(pieces))
+            ne = 1 if len(pieces) == 3 else 2
+            tr = []
+            for p in pieces:
+                for r in range(4):
+                    tr.append(RemoteDMATransfer(
+                        dst_ids=[_dst(topo, chip * 8 + 4 + r)], dma_engine_mask=((1 << ne) - 1) << (ne * len(tr)),
+                        remote_sem=T.sem.fin, srcs=[T.part[c * NP + p] for c in range(4)],
+                        dsts=[_piece(T.land, p)], alu_op=1))
+            g.remote_dma_fused(tr, local_sem=T.sem.sent)
+            g.wait_ge(T.sem.sent, len(tr) * ne)
+            return
+
+    q = {"1": g.sync, "2": g.sync, "3": g.scalar, "4": g.scalar}
+    for i in ("1", "3", "2", "4"):
+        a, b = ROWS[i]
+        q[i].dma_start(T.mine[a:b, :], T["x" + i][:]).then_inc(T.sem.loaded, 16)
+    g.wait_ge(T.sem.loaded, 64)
+    tr = []
+    for pieces, a_core, b_core in LANES:
+        for p in pieces:
+            tr.append(RemoteDMATransfer(
+                dst_ids=[_dst(topo, chip * 8 + a_core)], dma_engine_mask=0x3 << (2 * p),
+                remote_sem=T.sem.arr, src=_piece(T.mine, p), dst=T.slots[(k - 4) * NP + p]))
+    g.remote_dma_fused(tr, local_sem=T.sem.fin)
+    g.sync.wait_ge(T.sem.fin, 17)
+    g.scalar.wait_ge(T.sem.fin, 17)
+    for i in ("1", "3", "2", "4"):
+        a, b = ROWS[i]
+        q[i].dma_start(T["y" + i][:], T.land[a:b, :]).then_inc(T.sem.stored, 16)
+    g.wait_ge(T.sem.stored, 64)

@@ -1,17 +1,19 @@
 from concourse.bass import DstId, RemoteDMATransfer
 
-ROWS = {"1": (0, 192), "2": (192, 256), "3": (256, 512), "4": (512, 640)}
 CHIPS = (8, 9, 10, 11)
-NP = 5
-LANES = (((0, 1, 2), 2, 0), ((3, 4), 3, 1))
+XROWS = {"1": (0, 96), "2": (96, 128), "3": (128, 256), "4": (256, 320)}
+START = (0, 128, 192)
+YSRC = {"1": (0, 0, 96), "2": (0, 96, 128), "3": (1, 0, 128), "4": (2, 64, 128)}
+A_OF = (2, 3, 6)
+B_OF = (0, 1, 2)
 
 SCRATCH = {
-    "mine": ("dram", [640, 2], "float32"),
-    "slots": ("dram", [4 * NP, 128, 2], "float32"),
-    "part": ("dram", [4 * NP, 128, 2], "float32"),
-    "land": ("dram", [640, 2], "float32"),
+    "mine": ("dram", [320, 4], "float32"),
+    "slots": ("dram", [4, 128, 4], "float32"),
+    "part": ("dram", [4, 128, 4], "float32"),
+    "land": ("dram", [3, 128, 4], "float32"),
 }
-SEMAPHORES = ["loaded", "arr", "parr", "fin", "sent", "stored"]
+SEMAPHORES = ["loaded", "arr", "parr", "f0", "f1", "f2", "sent", "stored"]
 
 
 def _dst(topo, c):
@@ -19,60 +21,53 @@ def _dst(topo, c):
     return DstId(rid=rid, pnc=pid)
 
 
-def _piece(buf, p):
-    return buf[p * 128:(p + 1) * 128, :]
-
-
 def rank_program(g, core, T, topo):
     chip, k = topo.chip(core), core % 8
     if chip not in CHIPS:
         return
     ci = CHIPS.index(chip)
-    mate, plane, diag = chip ^ 1, chip ^ 2, chip ^ 3
+    is_rank = T.rank_of(core) is not None
+    sent = 0
 
-    for pieces, a_core, b_core in LANES:
-        if k == a_core:
-            g.wait_ge(T.sem.arr, 4 * len(pieces) * 2)
-            groups = ((diag, chip), (mate, plane)) if len(pieces) == 3 else ((diag,), (mate,), (plane,), (chip,))
-            tr = []
-            for p in pieces:
-                for grp in groups:
-                    tr.append(RemoteDMATransfer(
-                        dst_ids=[_dst(topo, c * 8 + b_core) for c in grp], dma_engine_mask=1 << len(tr),
-                        remote_sem=T.sem.parr, srcs=[T.slots[r * NP + p] for r in range(4)],
-                        dsts=[T.part[ci * NP + p] for c in grp], alu_op=1))
-            g.remote_dma_fused(tr, local_sem=T.sem.sent)
-            g.wait_ge(T.sem.sent, len(tr))
-            return
-        if k == b_core:
-            g.wait_ge(T.sem.parr, 4 * len(pieces))
-            ne = 1 if len(pieces) == 3 else 2
-            tr = []
-            for p in pieces:
-                for r in range(4):
-                    tr.append(RemoteDMATransfer(
-                        dst_ids=[_dst(topo, chip * 8 + 4 + r)], dma_engine_mask=((1 << ne) - 1) << (ne * len(tr)),
-                        remote_sem=T.sem.fin, srcs=[T.part[c * NP + p] for c in range(4)],
-                        dsts=[_piece(T.land, p)], alu_op=1))
-            g.remote_dma_fused(tr, local_sem=T.sem.sent)
-            g.wait_ge(T.sem.sent, len(tr) * ne)
-            return
+    if is_rank:
+        q = {"1": g.sync, "2": g.sync, "3": g.scalar, "4": g.scalar}
+        for i in ("1", "3", "2", "4"):
+            a, b = XROWS[i]
+            q[i].dma_start(T.mine[a:b, :], T["x" + i][:]).then_inc(T.sem.loaded, 16)
+        g.wait_ge(T.sem.loaded, 64)
+        tr = [RemoteDMATransfer(dst_ids=[_dst(topo, chip * 8 + A_OF[l])], dma_engine_mask=0xF << (4 * l),
+                                remote_sem=T.sem.arr, src=T.mine[START[l]:START[l] + 128, :], dst=T.slots[k - 4])
+              for l in range(3) if A_OF[l] != k]
+        g.remote_dma_fused(tr, local_sem=T.sem.sent)
+        sent += 4 * len(tr)
 
-    q = {"1": g.sync, "2": g.sync, "3": g.scalar, "4": g.scalar}
-    for i in ("1", "3", "2", "4"):
-        a, b = ROWS[i]
-        q[i].dma_start(T.mine[a:b, :], T["x" + i][:]).then_inc(T.sem.loaded, 16)
-    g.wait_ge(T.sem.loaded, 64)
-    tr = []
-    for pieces, a_core, b_core in LANES:
-        for p in pieces:
-            tr.append(RemoteDMATransfer(
-                dst_ids=[_dst(topo, chip * 8 + a_core)], dma_engine_mask=0x3 << (2 * p),
-                remote_sem=T.sem.arr, src=_piece(T.mine, p), dst=T.slots[(k - 4) * NP + p]))
-    g.remote_dma_fused(tr, local_sem=T.sem.fin)
-    g.sync.wait_ge(T.sem.fin, 17)
-    g.scalar.wait_ge(T.sem.fin, 17)
-    for i in ("1", "3", "2", "4"):
-        a, b = ROWS[i]
-        q[i].dma_start(T["y" + i][:], T.land[a:b, :]).then_inc(T.sem.stored, 16)
-    g.wait_ge(T.sem.stored, 64)
+    if k in A_OF:
+        l = A_OF.index(k)
+        srcs = [T.mine[START[l]:START[l] + 128, :] if r + 4 == k else T.slots[r] for r in range(4)]
+        g.wait_ge(T.sem.arr, 4 * (3 if is_rank else 4))
+        to = (chip ^ 3, chip ^ 1, chip ^ 2, chip)
+        g.remote_dma_fused(
+            [RemoteDMATransfer(dst_ids=[_dst(topo, c * 8 + B_OF[l]) for c in to], dma_engine_mask=0xFF,
+                               remote_sem=T.sem.parr, srcs=srcs, dsts=[T.part[ci] for c in to], alu_op=1)],
+            local_sem=T.sem.sent)
+        sent += 8
+
+    if k in B_OF:
+        l = B_OF.index(k)
+        g.wait_ge(T.sem.parr, 4 * 8)
+        g.remote_dma_fused(
+            [RemoteDMATransfer(dst_ids=[_dst(topo, chip * 8 + 4 + r) for r in range(4)], dma_engine_mask=0xFFFF,
+                               remote_sem=T.sem["f%d" % l], srcs=[T.part[c] for c in range(4)],
+                               dsts=[T.land[l] for r in range(4)], alu_op=1)],
+            local_sem=T.sem.sent)
+        sent += 16
+
+    if is_rank:
+        for i in ("1", "2", "3", "4"):
+            l, a, b = YSRC[i]
+            if i != "2":
+                q[i].wait_ge(T.sem["f%d" % l], 16)
+            q[i].dma_start(T["y" + i][:], T.land[l, a:b, :]).then_inc(T.sem.stored, 16)
+        g.wait_ge(T.sem.stored, 64)
+    if sent:
+        g.wait_ge(T.sem.sent, sent)

from concourse.bass import DstId, RemoteDMATransfer

CHIPS = (8, 9, 10, 11)
XROWS = {"1": (0, 96), "2": (96, 128), "3": (128, 256), "4": (256, 320)}
START = (0, 128, 192)
YSRC = {"1": (0, 0, 96), "2": (0, 96, 128), "3": (1, 0, 128), "4": (2, 64, 128)}
A_OF = (2, 3, 6)
B_OF = (0, 1, 2)

SCRATCH = {
    "mine": ("dram", [320, 4], "float32"),
    "slots": ("dram", [4, 128, 4], "float32"),
    "part": ("dram", [4, 128, 4], "float32"),
    "land": ("dram", [3, 128, 4], "float32"),
}
SEMAPHORES = ["loaded", "arr", "parr", "f0", "f1", "f2", "sent", "stored"]


def _dst(topo, c):
    rid, pid, _se = topo.addr(c)
    return DstId(rid=rid, pnc=pid)


def rank_program(g, core, T, topo):
    chip, k = topo.chip(core), core % 8
    if chip not in CHIPS:
        return
    ci = CHIPS.index(chip)
    is_rank = T.rank_of(core) is not None
    sent = 0

    if is_rank:
        q = {"1": g.sync, "2": g.sync, "3": g.scalar, "4": g.scalar}
        for i in ("1", "3", "2", "4"):
            a, b = XROWS[i]
            q[i].dma_start(T.mine[a:b, :], T["x" + i][:]).then_inc(T.sem.loaded, 16)
        g.wait_ge(T.sem.loaded, 64)
        tr = [RemoteDMATransfer(dst_ids=[_dst(topo, chip * 8 + A_OF[l])], dma_engine_mask=0xF << (4 * l),
                                remote_sem=T.sem.arr, src=T.mine[START[l]:START[l] + 128, :], dst=T.slots[k - 4])
              for l in range(3) if A_OF[l] != k]
        g.remote_dma_fused(tr, local_sem=T.sem.sent)
        sent += 4 * len(tr)

    if k in A_OF:
        l = A_OF.index(k)
        srcs = [T.mine[START[l]:START[l] + 128, :] if r + 4 == k else T.slots[r] for r in range(4)]
        g.wait_ge(T.sem.arr, 4 * (3 if is_rank else 4))
        to = (chip ^ 3, chip ^ 1, chip ^ 2, chip)
        g.remote_dma_fused(
            [RemoteDMATransfer(dst_ids=[_dst(topo, c * 8 + B_OF[l]) for c in to], dma_engine_mask=0xFF,
                               remote_sem=T.sem.parr, srcs=srcs, dsts=[T.part[ci] for c in to], alu_op=1)],
            local_sem=T.sem.sent)
        sent += 8

    if k in B_OF:
        l = B_OF.index(k)
        g.wait_ge(T.sem.parr, 4 * 8)
        g.remote_dma_fused(
            [RemoteDMATransfer(dst_ids=[_dst(topo, chip * 8 + 4 + r) for r in range(4)], dma_engine_mask=0xFFFF,
                               remote_sem=T.sem["f%d" % l], srcs=[T.part[c] for c in range(4)],
                               dsts=[T.land[l] for r in range(4)], alu_op=1)],
            local_sem=T.sem.sent)
        sent += 16

    if is_rank:
        for i in ("1", "2", "3", "4"):
            l, a, b = YSRC[i]
            if i != "2":
                q[i].wait_ge(T.sem["f%d" % l], 16)
            q[i].dma_start(T["y" + i][:], T.land[l, a:b, :]).then_inc(T.sem.stored, 16)
        g.wait_ge(T.sem.stored, 64)
    if sent:
        g.wait_ge(T.sem.sent, sent)
